import numpy as np
import ml_dtypes


def mxq(x, axis, fmt="e4m3"):
    dtype, down = {"e4m3": (ml_dtypes.float8_e4m3fn, 7), "e5m2": (ml_dtypes.float8_e5m2, 14)}[fmt]
    v = np.moveaxis(np.asarray(x, np.float32).astype(ml_dtypes.bfloat16).astype(np.float64), axis, -1)
    blocks = v.reshape(v.shape[:-1] + (-1, 32))
    amax = np.abs(blocks).max(-1, keepdims=True)
    byte = np.maximum(np.where(amax > 0, np.frexp(amax)[1] - 1 + 127, 0) - down, 1)
    scale = np.exp2(byte - 127.0)
    codes = (blocks / scale).astype(np.float32).astype(dtype).astype(np.float64)
    return np.moveaxis((codes * scale).reshape(v.shape), -1, axis)


WIDE = False


def mx_kscale(k):
    if not WIDE:
        return np.ones(k)
    levels = np.array([10, -10, 5, -5, 0])
    if k % 512:
        return np.exp2(np.random.permutation(np.resize(levels, k // 32))).repeat(32)
    a = np.empty((k // 512, 16))
    for p in range(k // 512):
        a[p, :8] = np.random.permutation(np.resize(levels, 8))
        for g in range(8):
            far = levels[np.abs(levels - a[p, g]) >= 10]
            a[p, g + 8] = far[np.random.randint(len(far))]
    return np.exp2(a.ravel()).repeat(32)


def f64(x):
    return np.asarray(x).astype(np.float64)


def striped(idx):
    return np.tile(idx.reshape(-1, 16).T, (8, 1)).astype(np.uint16)


def unstriped(offs):
    return offs[:16].T.reshape(-1).astype(np.int64)


E2M1 = np.array([0.0, 0.5, 1.0, 1.5, 2.0, 3.0, 4.0, 6.0, -0.0, -0.5, -1.0, -1.5, -2.0, -3.0, -4.0, -6.0])


def pack_weight(w, fmt):
    k, n = w.shape
    w = f64(np.asarray(w, np.float32).astype(ml_dtypes.bfloat16)).reshape(k // 32, 32, n)
    amax = np.abs(w).max(1)
    if fmt == "e4m3":
        byte = np.frexp(amax)[1] - 1 + 127 - 7
    else:
        mant, ex = np.frexp(amax / 6.0)
        byte = np.where(mant > 0.5, ex, ex - 1) + 127
    byte = np.clip(np.where(amax > 0, byte, 1), 1, 254)
    scaled = (w * np.exp2(127.0 - byte)[:, None, :]).reshape(k, n).astype(np.float32)
    by_word = np.ascontiguousarray(scaled.reshape(k // 512, 128, 4, n).transpose(0, 1, 3, 2))
    if fmt == "e4m3":
        words = by_word.astype(ml_dtypes.float8_e4m3fn).view(np.uint8)
    else:
        c = by_word.astype(ml_dtypes.float4_e2m1fn).view(np.uint8) & 0xF
        words = (c[..., 0::2] | (c[..., 1::2] << 4)).reshape(k // 512, 128, 2 * n)
    return np.ascontiguousarray(words), np.ascontiguousarray(byte.astype(np.uint8).reshape(k // 512, 16, n))


def unpack_weight(words, scales, fmt):
    g, _, n = scales.shape
    words = np.ascontiguousarray(words).reshape(g, 128, n, -1)
    if fmt == "e4m3":
        vals = words.view(ml_dtypes.float8_e4m3fn).astype(np.float64)
    else:
        nib = np.empty((g, 128, n, 4), np.uint8)
        nib[..., 0::2] = words & 0xF
        nib[..., 1::2] = words >> 4
        vals = E2M1[nib]
    vals = vals * np.repeat(np.exp2(scales.astype(np.float64) - 127.0), 8, axis=1)[..., None]
    return vals.transpose(0, 1, 3, 2).reshape(g * 512, n)


def gelu(v):
    return 0.5 * v * (1.0 + np.tanh(np.sqrt(2.0 / np.pi) * (v + 0.044715 * v**3)))


def bf(x):
    return np.asarray(x, np.float32).astype(ml_dtypes.bfloat16)


def planes(Y):
    n, m = Y.shape
    b = f64(bf(Y)).reshape(n // 32, 32, m)
    amax = np.abs(b).max(1)
    byte = np.clip(np.where(amax > 0, np.frexp(amax)[1] - 1 + 127 - 7, 1), 1, 254)
    codes = (b * np.exp2(127.0 - byte)[:, None, :]).reshape(n, m).astype(np.float32).astype(ml_dtypes.float8_e4m3fn).view(np.uint8)
    words = codes.reshape(n // 512, 128, 4, m).transpose(0, 1, 3, 2)
    return np.ascontiguousarray(words), np.ascontiguousarray(byte.astype(np.uint8).reshape(n // 512, 16, m))


K, H, N, T, S, P = 1024, 512, 1024, 4096, 1024, 512


def setup_inputs():
    n = np.random.standard_normal
    s = mx_kscale(K)[:, None]
    u = mx_kscale(H)[:, None]
    lam = np.exp(0.8 * n(N))
    d = {}
    d["tab_words"], d["tab_scales"] = pack_weight(n((K, T)) * s, "e4m3")
    d["offs"] = striped(np.random.permutation(T)[:S])
    d["wa"] = (n((K, H)) / K ** 0.5 / s).astype(np.float32)
    d["wb_words"], d["wb_scales"] = pack_weight(n((K, H)) / K ** 0.5 / s, "e2m1")
    d["gain"] = (np.exp(0.4 * n(H)) * u[:, 0]).astype(np.float32)
    d["w3"] = (n((H, N)) / H ** 0.5 / u * lam).astype(np.float32)
    d["thr"] = (0.5 * n(N) * lam).astype(np.float32)
    d["pos1"] = striped(np.random.permutation(S)[:P])
    d["pos2"] = striped(np.random.permutation(S)[:P])
    d["base"] = ((0.4 + 0.5 * n((N, P))) * lam[:, None]).astype(np.float32)
    return d


def reference(tab_words, tab_scales, offs, wa, wb_words, wb_scales, gain, w3, thr, pos1, pos2, base):
    v = unpack_weight(tab_words, tab_scales, "e4m3")[:, unstriped(offs)]
    a = mxq(f64(wa), 0, "e4m3").T @ v
    b = unpack_weight(wb_words, wb_scales, "e2m1").T @ v
    h = a * np.abs(b) * f64(gain)[:, None]
    x = (mxq(f64(w3), 0, "e4m3").T @ mxq(h, 0, "e4m3")) - f64(thr)[:, None]
    g2 = 0.5 * x * (1.0 + np.tanh(0.7978845608028654 * (x + 0.044715 * x ** 3)))
    y = g2[:, unstriped(pos1)] - np.maximum(g2[:, unstriped(pos2)], f64(base))
    words, scales = planes(y)
    return y, words, scales

@@ -1,0 +1,288 @@
+from contextlib import ExitStack
+
+import concourse.mybir as mybir
+
+K, H, N, T, S, M = 1024, 512, 1024, 4096, 1024, 512
+FLOPS = 2 * (2 * K * H * S + H * N * S)
+
+F32 = mybir.dt.float32
+BF16 = mybir.dt.bfloat16
+I32 = mybir.dt.int32
+U32 = mybir.dt.uint32
+U16 = mybir.dt.uint16
+U8 = mybir.dt.uint8
+FP8X4 = mybir.dt.float8_e4m3fn_x4
+FP4X4 = mybir.dt.float4_e2m1fn_x4
+ALU = mybir.AluOpType
+ACT = mybir.ActivationFunctionType
+P = 128
+
+
+def tile_list_block_face_features_kernel(
+    tc, tab_words, tab_scales, offs, wa, wb_words, wb_scales, gain, w3, thr, pos1, pos2, base, out_0, out_1, out_2
+):
+    nc = tc.nc
+    with ExitStack() as ctx:
+        keep = ctx.enter_context(tc.tile_pool(name="keep", bufs=1))
+        ring = ctx.enter_context(tc.tile_pool(name="ring", bufs=3))
+        psum = ctx.enter_context(tc.psum_pool(name="psum", bufs=1))
+
+        def held(shape, dtype, name):
+            return keep.tile(shape, dtype, name=name, align_bytes=64)
+
+        offs_t = held([P, S // 16], U16, "offs_t")
+        pos1_t = held([P, M // 16], U16, "pos1_t")
+        pos2_t = held([P, M // 16], U16, "pos2_t")
+        tab_w = [held([P, T], I32, f"tab_w{a}") for a in range(2)]
+        tab_s = held([P, 2, T], U8, "tab_s")
+        v_w = [held([P, S], U32, f"v_w{a}") for a in range(2)]
+        v_s = [held([P, S], U8, f"v_s{a}") for a in range(2)]
+        wb_w_raw = [held([P, 2 * H], U8, f"wb_w_raw{a}") for a in range(2)]
+        wb_s_raw = held([P, 2, H], U8, "wb_s_raw")
+        wb_w = held([P, 2, 2 * H], U8, "wb_w")
+        wb_s = held([P, 2, H], U8, "wb_s")
+        gain_t = held([P, 4], F32, "gain_t")
+        thr_t = held([P, 2, 4], F32, "thr_t")
+
+        nc.vector.memset(tab_s[:].rearrange("p a t -> p (a t)").bitcast(I32), 0)
+        nc.gpsimd.memset(wb_s_raw[:].rearrange("p a c -> p (a c)").bitcast(I32), 0)
+
+        tab_rows = [tab_words[a].rearrange("p t i -> p (t i)").bitcast(I32) for a in range(2)]
+        nc.sync.dma_start(out=tab_w[0][:], in_=tab_rows[0])
+        nc.sync.dma_start(offs_t[:], offs)
+        for a in range(2):
+            nc.scalar.dma_start(out=wb_w_raw[a][:].bitcast(I32), in_=wb_words[a].bitcast(I32))
+        nc.scalar.dma_start(out=gain_t[:], in_=gain.rearrange("(p t) -> p t", t=4))
+        nc.scalar.dma_start(out=thr_t[:], in_=thr.rearrange("(g p t) -> p g t", g=2, t=4))
+        for q in range(4):
+            nc.gpsimd.dma_start(
+                out=wb_s_raw[32 * q : 32 * q + 4, :, :].bitcast(I32),
+                in_=wb_scales[:, 4 * q : 4 * q + 4, :].rearrange("a r c -> r a c").bitcast(I32),
+            )
+        for q in range(4):
+            nc.gpsimd.dma_start(
+                out=tab_s[32 * q : 32 * q + 4, :, :].bitcast(I32),
+                in_=tab_scales[:, 4 * q : 4 * q + 4, :].rearrange("a r t -> r a t").bitcast(I32),
+            )
+        nc.sync.dma_start(out=tab_w[1][:, 0 : T // 2], in_=tab_rows[1][:, 0 : T // 2])
+        nc.sync.dma_start(out=tab_w[1][:, T // 2 : T], in_=tab_rows[1][:, T // 2 : T])
+
+        wa_parts = [(0, 0, H), (1, 0, H // 2), (1, H // 2, H)]
+        wa_raw = []
+        for a, c0, c1 in wa_parts:
+            raw = held([P, 4, c1 - c0], F32, f"wa_raw{a}_{c0}")
+            nc.sync.dma_start(out=raw[:], in_=wa[512 * a : 512 * (a + 1), c0:c1].rearrange("(p j) c -> p j c", j=4))
+            wa_raw.append(raw)
+        w3_raw = [[held([P, 2, 512], F32, f"w3_raw{g}_{u}") for u in range(2)] for g in range(2)]
+        base_t = [held([P, 4, M], F32, f"base{g}") for g in range(2)]
+        w3_rows = w3.rearrange("(p j) n -> p j n", j=4)
+        for g in range(2):
+            for u in range(2):
+                nc.sync.dma_start(out=w3_raw[g][u][:], in_=w3_rows[:, 2 * u : 2 * u + 2, 512 * g : 512 * (g + 1)])
+            if g == 0:
+                nc.sync.dma_start(pos2_t[:], pos2)
+                nc.sync.dma_start(pos1_t[:], pos1)
+            nc.sync.dma_start(out=base_t[g][:], in_=base[512 * g : 512 * (g + 1), :].rearrange("(p t) m -> p t m", t=4))
+
+        sign_01 = held([P, 4], F32, "sign_01")
+        sign_t = held([P, 4], F32, "sign_t")
+        neg_thr = held([P, 2, 4], F32, "neg_thr")
+        nc.gpsimd.tensor_scalar(out=sign_01[:], in0=gain_t[:], scalar1=0.0, scalar2=2.0, op0=ALU.is_ge, op1=ALU.mult)
+        nc.gpsimd.tensor_scalar(out=sign_t[:], in0=sign_01[:], scalar1=1.0, scalar2=-1.0, op0=ALU.mult, op1=ALU.add)
+        nc.gpsimd.tensor_scalar(out=neg_thr[:], in0=thr_t[:], scalar1=-1.0, scalar2=0.0, op0=ALU.mult, op1=ALU.add)
+
+        for a in range(2):
+            nc.vector.tensor_copy(
+                out=wb_w[:, a, :].rearrange("p (t m b) -> p m t b", t=4, b=2),
+                in_=wb_w_raw[a][:].rearrange("p (m t b) -> p m t b", t=4, b=2),
+            )
+        nc.vector.tensor_copy(out=v_w[0][:], in_=tab_w[0][:].bitcast(U32).indirect(offs_t[:]))
+        for a in range(2):
+            nc.vector.tensor_copy(out=v_s[a][:], in_=tab_s[:, a, :].indirect(offs_t[:]))
+        nc.vector.tensor_copy(
+            out=wb_s[:].rearrange("p a (t m) -> p a m t", t=4), in_=wb_s_raw[:].rearrange("p a (m t) -> p a m t", t=4)
+        )
+        for half in range(2):
+            nc.vector.tensor_copy(
+                out=v_w[1][:, 512 * half : 512 * (half + 1)],
+                in_=tab_w[1][:].bitcast(U32).indirect(offs_t[:, 32 * half : 32 * (half + 1)]),
+            )
+
+        abs_b = [held([P, 4, 512], F32, f"abs_b{half}") for half in range(2)]
+        for half in range(2):
+            cols = slice(512 * half, 512 * (half + 1))
+            for t in range(4):
+                bank = psum.tile([P, 512], F32, name="bank_b", bufs=2)
+                for a in range(2):
+                    nc.tensor.matmul_mx(
+                        out=bank[:],
+                        lhsT=wb_w[:, a, 256 * t : 256 * (t + 1)].bitcast(FP4X4),
+                        lhsT_scale=wb_s[:, a, 128 * t : 128 * (t + 1)],
+                        rhs=v_w[a][:, cols].bitcast(FP8X4),
+                        rhs_scale=v_s[a][:, cols],
+                        start=(a == 0),
+                        stop=(a == 1),
+                    )
+                nc.scalar.activation(out=abs_b[half][:, t, :], in_=bank[:], func=ACT.Abs, scale=gain_t[:, t : t + 1])
+
+        wa_bf = [held([P, 4 * H], BF16, "staging") for a in range(2)]
+        wa_w = [held([P, H], U32, f"wa_w{a}") for a in range(2)]
+        wa_s = [held([P, H], U8, f"wa_s{a}") for a in range(2)]
+        for (a, c0, c1), raw in zip(wa_parts, wa_raw):
+            nc.vector.tensor_copy(
+                out=wa_bf[a][:].rearrange("p (u e m j) -> p u m j e", u=2, e=2, j=4)[:, :, c0 // 4 : c1 // 4, :, :],
+                in_=raw[:].rearrange("p j (m u e) -> p u m j e", u=2, e=2),
+            )
+            if c1 == H:
+                for t in range(4):
+                    nc.vector.quantize_mx(
+                        out=wa_w[a][:, 128 * t : 128 * (t + 1)].bitcast(FP8X4),
+                        scales=wa_s[a][:, 128 * t : 128 * (t + 1)],
+                        in_=wa_bf[a][:, 512 * t : 512 * (t + 1)],
+                    )
+
+        w3_w = [held([P, 512], U32, f"w3_w{g}") for g in range(2)]
+        w3_s = [held([P, 512], U8, f"w3_s{g}") for g in range(2)]
+
+        def prepare_w3(g):
+            signed = held([P, 4, 512], BF16, "staging")
+            woven = keep.tile([P, 2048], BF16, name="w3_woven", align_bytes=64)
+            for j in range(4):
+                nc.scalar.activation(
+                    out=signed[:, j, :].rearrange("p (u e m) -> p u m e", u=2, e=2),
+                    in_=w3_raw[g][j // 2][:, j % 2, :].rearrange("p (m u e) -> p u m e", u=2, e=2),
+                    func=ACT.Copy,
+                    scale=sign_t[:, j : j + 1],
+                )
+            nc.scalar.copy(
+                out=woven[:].rearrange("p (c i j) -> p c j i", i=4, j=4),
+                in_=signed[:].rearrange("p j (c i) -> p c j i", i=4),
+            )
+            nc.vector.quantize_mx(out=w3_w[g][:].bitcast(FP8X4), scales=w3_s[g][:], in_=woven[:])
+
+        h_w = held([P, S], U32, "h_w")
+        h_s = held([P, S], U8, "h_s")
+        h_bf = []
+
+        def quantise_h(c):
+            cols = slice(128 * c, 128 * (c + 1))
+            nc.vector.quantize_mx(out=h_w[:, cols].bitcast(FP8X4), scales=h_s[:, cols], in_=h_bf[c][:])
+
+        for c in range(8):
+            cols = slice(128 * c, 128 * (c + 1))
+            bank = psum.tile([P, 4, 128], F32, name="bank_a", bufs=4)
+            for a in range(2):
+                for t in range(4):
+                    nc.tensor.matmul_mx(
+                        out=bank[:, t, :],
+                        lhsT=wa_w[a][:, 128 * t : 128 * (t + 1)].bitcast(FP8X4),
+                        lhsT_scale=wa_s[a][:, 128 * t : 128 * (t + 1)],
+                        rhs=v_w[a][:, cols].bitcast(FP8X4),
+                        rhs_scale=v_s[a][:, cols],
+                        start=(a == 0 and t == 0),
+                        stop=(a == 1 and t == 3),
+                    )
+            h_bf.append(ring.tile([P, 512], BF16, name="h_bf", align_bytes=64))
+            in_half = slice(128 * (c % 4), 128 * (c % 4 + 1))
+            nc.vector.tensor_tensor(
+                out=h_bf[c][:].rearrange("p (n i t) -> p n t i", i=2, t=4),
+                in0=bank[:].rearrange("p t (n i) -> p n t i", i=2),
+                in1=abs_b[c // 4][:, :, in_half].rearrange("p t (n i) -> p n t i", i=2),
+                op=ALU.mult,
+            )
+            if c > 0:
+                quantise_h(c - 1)
+            if c == 5:
+                prepare_w3(0)
+        quantise_h(7)
+
+        g2 = {}
+
+        def second_stage(g, t):
+            g2[g, t] = keep.tile([P, S], F32, name="g2", bufs=6)
+            for half in range(2):
+                cols = slice(512 * half, 512 * (half + 1))
+                bank = psum.tile([P, 512], F32, name="bank_x", bufs=2)
+                nc.tensor.matmul_mx(
+                    out=bank[:],
+                    lhsT=w3_w[g][:, 128 * t : 128 * (t + 1)].bitcast(FP8X4),
+                    lhsT_scale=w3_s[g][:, 128 * t : 128 * (t + 1)],
+                    rhs=h_w[:, cols].bitcast(FP8X4),
+                    rhs_scale=h_s[:, cols],
+                    start=True,
+                    stop=True,
+                )
+                nc.scalar.activation(
+                    out=g2[g, t][:, cols], in_=bank[:], func=ACT.Gelu_apprx_tanh, bias=neg_thr[:, g, t : t + 1]
+                )
+
+        y_w = held([P, 2, M], U32, "y_w")
+        y_s = held([P, 2, M], U8, "y_s")
+        pieces = [(0, 0, 512), (1, 0, 256), (1, 256, 512)]
+        y = [held([P, 4, m1 - m0], F32, f"y{g}_{m0}") for g, m0, m1 in pieces]
+        larger = {}
+
+        def pick_partner(k, t):
+            g, m0, m1 = pieces[k]
+            larger[k, t] = ring.tile([P, m1 - m0], F32, name="larger")
+            nc.vector.tensor_copy(out=larger[k, t][:], in_=g2[g, t][:].indirect(pos2_t[:, m0 // 16 : m1 // 16]))
+
+        def take_max(k, t):
+            g, m0, m1 = pieces[k]
+            nc.vector.tensor_tensor(out=larger[k, t][:], in0=larger[k, t][:], in1=base_t[g][:, t, m0:m1], op=ALU.max)
+
+        def finish(k, t):
+            g, m0, m1 = pieces[k]
+            nc.vector.tensor_tensor(
+                out=y[k][:, t, :], in0=g2[g, t][:].indirect(pos1_t[:, m0 // 16 : m1 // 16]), in1=larger[k, t][:], op=ALU.subtract
+            )
+            rows = out_0[512 * g : 512 * (g + 1), m0:m1].rearrange("(p t) m -> p t m", t=4)
+            nc.sync.dma_start(out=rows[:, t, :], in_=y[k][:, t, :])
+
+        y_bf = {}
+
+        def round_y(k):
+            g, m0, m1 = pieces[k]
+            y_bf[k] = held([P, 4 * (m1 - m0)], BF16, f"y_bf{k}")
+            dst = y_bf[k][:].rearrange("p (c i t) -> p c t i", i=2, t=4)
+            src = y[k][:].rearrange("p t (c i) -> p c t i", i=2)
+            if k == len(pieces) - 1:
+                nc.vector.tensor_copy(out=dst, in_=src)
+            else:
+                nc.scalar.copy(out=dst, in_=src)
+
+        def quantise_y(k):
+            g, m0, m1 = pieces[k]
+            nc.vector.quantize_mx(out=y_w[:, g, m0:m1].bitcast(FP8X4), scales=y_s[:, g, m0:m1], in_=y_bf[k][:])
+            words = out_1[g].rearrange("p m t -> p (m t)").bitcast(I32)
+            nc.sync.dma_start(out=words[:, m0:m1], in_=y_w[:, g, m0:m1].bitcast(I32))
+
+        for t in range(2):
+            second_stage(0, t)
+        prepare_w3(1)
+        for t in range(2, 4):
+            second_stage(0, t)
+        for t in range(2):
+            second_stage(1, t)
+
+        steps = [(k, t) for k in range(len(pieces)) for t in range(4)]
+        for i, (k, t) in enumerate(steps):
+            pick_partner(k, t)
+            if i > 0:
+                finish(*steps[i - 1])
+            take_max(k, t)
+            if i in (1, 2):
+                second_stage(1, i + 1)
+            if k > 0 and t == 0:
+                round_y(k - 1)
+            if k > 0 and t == 3:
+                quantise_y(k - 1)
+        finish(*steps[-1])
+        round_y(len(pieces) - 1)
+        quantise_y(len(pieces) - 1)
+        for q in range(4):
+            queue = nc.scalar if q % 2 else nc.sync
+            queue.dma_start(
+                out=out_2[:, 4 * q : 4 * q + 4, :].rearrange("g r m -> r g m").bitcast(I32),
+                in_=y_s[32 * q : 32 * q + 4, :, :].bitcast(I32),
+            )

@@ -25,22 +25,26 @@ def tile_list_block_face_features_kernel(
     with ExitStack() as ctx:
         keep = ctx.enter_context(tc.tile_pool(name="keep", bufs=1))
         ring = ctx.enter_context(tc.tile_pool(name="ring", bufs=3))
+        loads = ctx.enter_context(tc.tile_pool(name="loads", bufs=1))
         psum = ctx.enter_context(tc.psum_pool(name="psum", bufs=1))
 
         def held(shape, dtype, name):
             return keep.tile(shape, dtype, name=name, align_bytes=64)
 
+        def landed(shape, dtype, name, kib):
+            return loads.tile(shape, dtype, name=name, offset=1024 * kib, align_bytes=64)
+
         offs_t = held([P, S // 16], U16, "offs_t")
         pos1_t = held([P, M // 16], U16, "pos1_t")
         pos2_t = held([P, M // 16], U16, "pos2_t")
-        tab_w = [held([P, T], I32, f"tab_w{a}") for a in range(2)]
-        tab_s = held([P, 2, T], U8, "tab_s")
+        wb_w_raw = landed([P, 2, 2 * H], U8, "wb_w_raw", 31)
+        tab_w = [landed([P, T], I32, f"tab_w{a}", 16 * a) for a in range(2)]
+        tab_s = landed([P, 2, T], U8, "tab_s", 40)
         v_w = [held([P, S], U32, f"v_w{a}") for a in range(2)]
-        v_s = [held([P, S], U8, f"v_s{a}") for a in range(2)]
-        wb_w_raw = [held([P, 2 * H], U8, f"wb_w_raw{a}") for a in range(2)]
+        v_s = [landed([P, S], U8, f"v_s{a}", a) for a in range(2)]
         wb_s_raw = held([P, 2, H], U8, "wb_s_raw")
         wb_w = held([P, 2, 2 * H], U8, "wb_w")
-        wb_s = held([P, 2, H], U8, "wb_s")
+        wb_s = landed([P, 2, H], U8, "wb_s", 47)
         gain_t = held([P, 4], F32, "gain_t")
         thr_t = held([P, 2, 4], F32, "thr_t")
 
@@ -48,55 +52,58 @@ def tile_list_block_face_features_kernel(
         nc.gpsimd.memset(wb_s_raw[:].rearrange("p a c -> p (a c)").bitcast(I32), 0)
 
         tab_rows = [tab_words[a].rearrange("p t i -> p (t i)").bitcast(I32) for a in range(2)]
-        nc.sync.dma_start(out=tab_w[0][:], in_=tab_rows[0])
         nc.sync.dma_start(offs_t[:], offs)
-        for a in range(2):
-            nc.scalar.dma_start(out=wb_w_raw[a][:].bitcast(I32), in_=wb_words[a].bitcast(I32))
-        nc.scalar.dma_start(out=gain_t[:], in_=gain.rearrange("(p t) -> p t", t=4))
-        nc.scalar.dma_start(out=thr_t[:], in_=thr.rearrange("(g p t) -> p g t", g=2, t=4))
+        nc.scalar.dma_start(out=wb_w_raw[:].bitcast(I32), in_=wb_words.rearrange("a p c -> p a c").bitcast(I32))
+        nc.gpsimd.dma_start(out=gain_t[:], in_=gain.rearrange("(p t) -> p t", t=4))
+        nc.gpsimd.dma_start(out=thr_t[:], in_=thr.rearrange("(g p t) -> p g t", g=2, t=4))
+        nc.sync.dma_start(pos2_t[:], pos2)
+        nc.sync.dma_start(pos1_t[:], pos1)
+        wa_parts = [(0, 0, H, 32), (1, 0, H // 2, 2), (1, H // 2, H, 6)]
+        wa_raw = [landed([P, 4, c1 - c0], F32, f"wa_raw{a}_{c0}", kib) for a, c0, c1, kib in wa_parts]
+        wa_bf = [landed([P, 4 * H], BF16, f"wa_bf{a}", 16) for a in range(2)]
+        wa_w = [held([P, H], U32, f"wa_w{a}") for a in range(2)]
+        wa_s = [held([P, H], U8, f"wa_s{a}") for a in range(2)]
+
+        def load_wa(i):
+            a, c0, c1, kib = wa_parts[i]
+            rows = wa[512 * a : 512 * (a + 1), c0:c1].rearrange("(p j) c -> p j c", j=4)
+            nc.sync.dma_start(out=wa_raw[i][:], in_=rows)
+
+        def prepare_wa(i):
+            a, c0, c1, kib = wa_parts[i]
+            nc.vector.tensor_copy(
+                out=wa_bf[a][:].rearrange("p (u e m j) -> p u m j e", u=2, e=2, j=4)[:, :, c0 // 4 : c1 // 4, :, :],
+                in_=wa_raw[i][:].rearrange("p j (m u e) -> p u m j e", u=2, e=2),
+            )
+            if c1 == H:
+                for t in range(4):
+                    nc.vector.quantize_mx(
+                        out=wa_w[a][:, 128 * t : 128 * (t + 1)].bitcast(FP8X4),
+                        scales=wa_s[a][:, 128 * t : 128 * (t + 1)],
+                        in_=wa_bf[a][:, 512 * t : 512 * (t + 1)],
+                    )
+
+        nc.sync.dma_start(out=tab_w[0][:], in_=tab_rows[0])
         for q in range(4):
-            nc.gpsimd.dma_start(
+            nc.scalar.dma_start(
                 out=wb_s_raw[32 * q : 32 * q + 4, :, :].bitcast(I32),
                 in_=wb_scales[:, 4 * q : 4 * q + 4, :].rearrange("a r c -> r a c").bitcast(I32),
             )
         for q in range(4):
-            nc.gpsimd.dma_start(
+            nc.sync.dma_start(
                 out=tab_s[32 * q : 32 * q + 4, :, :].bitcast(I32),
                 in_=tab_scales[:, 4 * q : 4 * q + 4, :].rearrange("a r t -> r a t").bitcast(I32),
             )
-        nc.sync.dma_start(out=tab_w[1][:, 0 : T // 2], in_=tab_rows[1][:, 0 : T // 2])
-        nc.sync.dma_start(out=tab_w[1][:, T // 2 : T], in_=tab_rows[1][:, T // 2 : T])
-
-        wa_parts = [(0, 0, H), (1, 0, H // 2), (1, H // 2, H)]
-        wa_raw = []
-        for a, c0, c1 in wa_parts:
-            raw = held([P, 4, c1 - c0], F32, f"wa_raw{a}_{c0}")
-            nc.sync.dma_start(out=raw[:], in_=wa[512 * a : 512 * (a + 1), c0:c1].rearrange("(p j) c -> p j c", j=4))
-            wa_raw.append(raw)
-        w3_raw = [[held([P, 2, 512], F32, f"w3_raw{g}_{u}") for u in range(2)] for g in range(2)]
-        base_t = [held([P, 4, M], F32, f"base{g}") for g in range(2)]
-        w3_rows = w3.rearrange("(p j) n -> p j n", j=4)
-        for g in range(2):
-            for u in range(2):
-                nc.sync.dma_start(out=w3_raw[g][u][:], in_=w3_rows[:, 2 * u : 2 * u + 2, 512 * g : 512 * (g + 1)])
-            if g == 0:
-                nc.sync.dma_start(pos2_t[:], pos2)
-                nc.sync.dma_start(pos1_t[:], pos1)
-            nc.sync.dma_start(out=base_t[g][:], in_=base[512 * g : 512 * (g + 1), :].rearrange("(p t) m -> p t m", t=4))
-
-        sign_01 = held([P, 4], F32, "sign_01")
-        sign_t = held([P, 4], F32, "sign_t")
-        neg_thr = held([P, 2, 4], F32, "neg_thr")
-        nc.gpsimd.tensor_scalar(out=sign_01[:], in0=gain_t[:], scalar1=0.0, scalar2=2.0, op0=ALU.is_ge, op1=ALU.mult)
-        nc.gpsimd.tensor_scalar(out=sign_t[:], in0=sign_01[:], scalar1=1.0, scalar2=-1.0, op0=ALU.mult, op1=ALU.add)
-        nc.gpsimd.tensor_scalar(out=neg_thr[:], in0=thr_t[:], scalar1=-1.0, scalar2=0.0, op0=ALU.mult, op1=ALU.add)
-
         for a in range(2):
             nc.vector.tensor_copy(
                 out=wb_w[:, a, :].rearrange("p (t m b) -> p m t b", t=4, b=2),
-                in_=wb_w_raw[a][:].rearrange("p (m t b) -> p m t b", t=4, b=2),
+                in_=wb_w_raw[:, a, :].rearrange("p (m t b) -> p m t b", t=4, b=2),
             )
+        nc.sync.dma_start(out=tab_w[1][:], in_=tab_rows[1])
+        load_wa(0)
         nc.vector.tensor_copy(out=v_w[0][:], in_=tab_w[0][:].bitcast(U32).indirect(offs_t[:]))
+        load_wa(1)
+        load_wa(2)
         for a in range(2):
             nc.vector.tensor_copy(out=v_s[a][:], in_=tab_s[:, a, :].indirect(offs_t[:]))
         nc.vector.tensor_copy(
@@ -108,11 +115,26 @@ def tile_list_block_face_features_kernel(
                 in_=tab_w[1][:].bitcast(U32).indirect(offs_t[:, 32 * half : 32 * (half + 1)]),
             )
 
+        w3_raw = [[landed([P, 2, 512], F32, f"w3_raw{g}_{u}", [[10, 40], [20, 24]][g][u]) for u in range(2)] for g in range(2)]
+        base_t = [landed([P, 4, M], F32, f"base{g}", 32 - 30 * g) for g in range(2)]
+        w3_rows = w3.rearrange("(p j) n -> p j n", j=4)
+        for g in range(2):
+            for u in range(2):
+                nc.sync.dma_start(out=w3_raw[g][u][:], in_=w3_rows[:, 2 * u : 2 * u + 2, 512 * g : 512 * (g + 1)])
+            nc.sync.dma_start(out=base_t[g][:], in_=base[512 * g : 512 * (g + 1), :].rearrange("(p t) m -> p t m", t=4))
+
+        sign_01 = held([P, 4], F32, "sign_01")
+        sign_t = held([P, 4], F32, "sign_t")
+        neg_thr = held([P, 2, 4], F32, "neg_thr")
+        nc.gpsimd.tensor_scalar(out=sign_01[:], in0=gain_t[:], scalar1=0.0, scalar2=2.0, op0=ALU.is_ge, op1=ALU.mult)
+        nc.gpsimd.tensor_scalar(out=sign_t[:], in0=sign_01[:], scalar1=1.0, scalar2=-1.0, op0=ALU.mult, op1=ALU.add)
+        nc.gpsimd.tensor_scalar(out=neg_thr[:], in0=thr_t[:], scalar1=-1.0, scalar2=0.0, op0=ALU.mult, op1=ALU.add)
+
         abs_b = [held([P, 4, 512], F32, f"abs_b{half}") for half in range(2)]
         for half in range(2):
             cols = slice(512 * half, 512 * (half + 1))
             for t in range(4):
-                bank = psum.tile([P, 512], F32, name="bank_b", bufs=2)
+                bank = psum.tile([P, 512], F32, name="bank", bufs=8)
                 for a in range(2):
                     nc.tensor.matmul_mx(
                         out=bank[:],
@@ -125,27 +147,14 @@ def tile_list_block_face_features_kernel(
                     )
                 nc.scalar.activation(out=abs_b[half][:, t, :], in_=bank[:], func=ACT.Abs, scale=gain_t[:, t : t + 1])
 
-        wa_bf = [held([P, 4 * H], BF16, "staging") for a in range(2)]
-        wa_w = [held([P, H], U32, f"wa_w{a}") for a in range(2)]
-        wa_s = [held([P, H], U8, f"wa_s{a}") for a in range(2)]
-        for (a, c0, c1), raw in zip(wa_parts, wa_raw):
-            nc.vector.tensor_copy(
-                out=wa_bf[a][:].rearrange("p (u e m j) -> p u m j e", u=2, e=2, j=4)[:, :, c0 // 4 : c1 // 4, :, :],
-                in_=raw[:].rearrange("p j (m u e) -> p u m j e", u=2, e=2),
-            )
-            if c1 == H:
-                for t in range(4):
-                    nc.vector.quantize_mx(
-                        out=wa_w[a][:, 128 * t : 128 * (t + 1)].bitcast(FP8X4),
-                        scales=wa_s[a][:, 128 * t : 128 * (t + 1)],
-                        in_=wa_bf[a][:, 512 * t : 512 * (t + 1)],
-                    )
+        for i in range(3):
+            prepare_wa(i)
 
         w3_w = [held([P, 512], U32, f"w3_w{g}") for g in range(2)]
         w3_s = [held([P, 512], U8, f"w3_s{g}") for g in range(2)]
 
         def prepare_w3(g):
-            signed = held([P, 4, 512], BF16, "staging")
+            signed = landed([P, 4, 512], BF16, f"w3_signed{g}", 44)
             woven = keep.tile([P, 2048], BF16, name="w3_woven", align_bytes=64)
             for j in range(4):
                 nc.scalar.activation(
@@ -158,7 +167,12 @@ def tile_list_block_face_features_kernel(
                 out=woven[:].rearrange("p (c i j) -> p c j i", i=4, j=4),
                 in_=signed[:].rearrange("p j (c i) -> p c j i", i=4),
             )
+            return woven
+
+        def quantise_w3(g, woven):
             nc.vector.quantize_mx(out=w3_w[g][:].bitcast(FP8X4), scales=w3_s[g][:], in_=woven[:])
+
+        woven0 = prepare_w3(0)
 
         h_w = held([P, S], U32, "h_w")
         h_s = held([P, S], U8, "h_s")
@@ -170,7 +184,7 @@ def tile_list_block_face_features_kernel(
 
         for c in range(8):
             cols = slice(128 * c, 128 * (c + 1))
-            bank = psum.tile([P, 4, 128], F32, name="bank_a", bufs=4)
+            bank = psum.tile([P, 4, 128], F32, name="bank", bufs=8)
             for a in range(2):
                 for t in range(4):
                     nc.tensor.matmul_mx(
@@ -192,9 +206,11 @@ def tile_list_block_face_features_kernel(
             )
             if c > 0:
                 quantise_h(c - 1)
-            if c == 5:
-                prepare_w3(0)
+        quantise_w3(0, woven0)
         quantise_h(7)
+        probe = held([P, 2], U32, "probe")
+        nc.gpsimd.tensor_copy(out=probe[:, 0:1], in_=wa_w[1][:, 511:512])
+        nc.gpsimd.tensor_copy(out=probe[:, 1:2], in_=h_w[:, 1023:1024])
 
         g2 = {}
 
@@ -202,7 +218,7 @@ def tile_list_block_face_features_kernel(
             g2[g, t] = keep.tile([P, S], F32, name="g2", bufs=6)
             for half in range(2):
                 cols = slice(512 * half, 512 * (half + 1))
-                bank = psum.tile([P, 512], F32, name="bank_x", bufs=2)
+                bank = psum.tile([P, 512], F32, name="bank", bufs=8)
                 nc.tensor.matmul_mx(
                     out=bank[:],
                     lhsT=w3_w[g][:, 128 * t : 128 * (t + 1)].bitcast(FP8X4),
@@ -259,7 +275,7 @@ def tile_list_block_face_features_kernel(
 
         for t in range(2):
             second_stage(0, t)
-        prepare_w3(1)
+        quantise_w3(1, prepare_w3(1))
         for t in range(2, 4):
             second_stage(0, t)
         for t in range(2):

@@ -39,17 +39,18 @@ def tile_list_block_face_features_kernel(
         pos2_t = held([P, M // 16], U16, "pos2_t")
         wb_w_raw = landed([P, 2, 2 * H], U8, "wb_w_raw", 31)
         tab_w = [landed([P, T], I32, f"tab_w{a}", 16 * a) for a in range(2)]
-        tab_s = landed([P, 2, T], U8, "tab_s", 40)
+        tab_s = landed([P, T], U8, "tab_s", 40)
         v_w = [held([P, S], U32, f"v_w{a}") for a in range(2)]
-        v_s = [landed([P, S], U8, f"v_s{a}", a) for a in range(2)]
+        v_s = [landed([P, S], U8, "v_s0", 0), held([P, S], U8, "v_s1")]
         wb_s_raw = held([P, 2, H], U8, "wb_s_raw")
         wb_w = held([P, 2, 2 * H], U8, "wb_w")
-        wb_s = landed([P, 2, H], U8, "wb_s", 47)
+        wb_s = landed([P, 2, H], U8, "wb_s", 1)
         gain_t = held([P, 4], F32, "gain_t")
         thr_t = held([P, 2, 4], F32, "thr_t")
 
-        nc.vector.memset(tab_s[:].rearrange("p a t -> p (a t)").bitcast(I32), 0)
+        nc.vector.memset(tab_s[:].bitcast(I32), 0)
         nc.gpsimd.memset(wb_s_raw[:].rearrange("p a c -> p (a c)").bitcast(I32), 0)
+        nc.gpsimd.memset(v_s[1][:].bitcast(I32), 0)
 
         tab_rows = [tab_words[a].rearrange("p t i -> p (t i)").bitcast(I32) for a in range(2)]
         nc.sync.dma_start(offs_t[:], offs)
@@ -83,40 +84,43 @@ def tile_list_block_face_features_kernel(
                         in_=wa_bf[a][:, 512 * t : 512 * (t + 1)],
                     )
 
-        nc.sync.dma_start(out=tab_w[0][:], in_=tab_rows[0])
         for q in range(4):
-            nc.scalar.dma_start(
+            if q == 2:
+                nc.sync.dma_start(out=tab_w[0][:], in_=tab_rows[0])
+            nc.sync.dma_start(
                 out=wb_s_raw[32 * q : 32 * q + 4, :, :].bitcast(I32),
                 in_=wb_scales[:, 4 * q : 4 * q + 4, :].rearrange("a r c -> r a c").bitcast(I32),
             )
         for q in range(4):
             nc.sync.dma_start(
-                out=tab_s[32 * q : 32 * q + 4, :, :].bitcast(I32),
-                in_=tab_scales[:, 4 * q : 4 * q + 4, :].rearrange("a r t -> r a t").bitcast(I32),
+                out=tab_s[32 * q : 32 * q + 8, :].bitcast(I32), in_=tab_scales[:, 4 * q : 4 * q + 4, :].bitcast(I32)
             )
         for a in range(2):
             nc.vector.tensor_copy(
-                out=wb_w[:, a, :].rearrange("p (t m b) -> p m t b", t=4, b=2),
-                in_=wb_w_raw[:, a, :].rearrange("p (m t b) -> p m t b", t=4, b=2),
+                out=wb_w[:, a, :].rearrange("p (t m b) -> p t m b", t=4, b=2),
+                in_=wb_w_raw[:, a, :].rearrange("p (m t b) -> p t m b", t=4, b=2),
             )
         nc.sync.dma_start(out=tab_w[1][:], in_=tab_rows[1])
         load_wa(0)
         nc.vector.tensor_copy(out=v_w[0][:], in_=tab_w[0][:].bitcast(U32).indirect(offs_t[:]))
         load_wa(1)
         load_wa(2)
-        for a in range(2):
-            nc.vector.tensor_copy(out=v_s[a][:], in_=tab_s[:, a, :].indirect(offs_t[:]))
         nc.vector.tensor_copy(
-            out=wb_s[:].rearrange("p a (t m) -> p a m t", t=4), in_=wb_s_raw[:].rearrange("p a (m t) -> p a m t", t=4)
+            out=wb_s[:].rearrange("p a (t m) -> p a t m", t=4), in_=wb_s_raw[:].rearrange("p a (m t) -> p a t m", t=4)
         )
+        nc.vector.tensor_copy(out=v_s[0][:], in_=tab_s[:].indirect(offs_t[:]))
+        for q in range(4):
+            nc.scalar.dma_start(
+                out=v_s[1][32 * q : 32 * q + 4, :].bitcast(I32), in_=v_s[0][32 * q + 4 : 32 * q + 8, :].bitcast(I32)
+            )
         for half in range(2):
             nc.vector.tensor_copy(
                 out=v_w[1][:, 512 * half : 512 * (half + 1)],
                 in_=tab_w[1][:].bitcast(U32).indirect(offs_t[:, 32 * half : 32 * (half + 1)]),
             )
 
-        w3_raw = [[landed([P, 2, 512], F32, f"w3_raw{g}_{u}", [[10, 40], [20, 24]][g][u]) for u in range(2)] for g in range(2)]
-        base_t = [landed([P, 4, M], F32, f"base{g}", 32 - 30 * g) for g in range(2)]
+        w3_raw = [[landed([P, 2, 512], F32, f"w3_raw{g}_{u}", [[40, 28], [20, 24]][g][u]) for u in range(2)] for g in range(2)]
+        base_t = [landed([P, 4, M], F32, f"base{g}", 32 - 26 * g) for g in range(2)]
         w3_rows = w3.rearrange("(p j) n -> p j n", j=4)
         for g in range(2):
             for u in range(2):
@@ -154,7 +158,7 @@ def tile_list_block_face_features_kernel(
         w3_s = [held([P, 512], U8, f"w3_s{g}") for g in range(2)]
 
         def prepare_w3(g):
-            signed = landed([P, 4, 512], BF16, f"w3_signed{g}", 44)
+            signed = landed([P, 4, 512], BF16, f"w3_signed{g}", 1)
             woven = keep.tile([P, 2048], BF16, name="w3_woven", align_bytes=64)
             for j in range(4):
                 nc.scalar.activation(
@@ -208,9 +212,6 @@ def tile_list_block_face_features_kernel(
                 quantise_h(c - 1)
         quantise_w3(0, woven0)
         quantise_h(7)
-        probe = held([P, 2], U32, "probe")
-        nc.gpsimd.tensor_copy(out=probe[:, 0:1], in_=wa_w[1][:, 511:512])
-        nc.gpsimd.tensor_copy(out=probe[:, 1:2], in_=h_w[:, 1023:1024])
 
         g2 = {}
 

@@ -154,12 +154,12 @@ def tile_list_block_face_features_kernel(
         for i in range(3):
             prepare_wa(i)
 
-        w3_w = [held([P, 512], U32, f"w3_w{g}") for g in range(2)]
+        w3_w = [landed([P, 512], U32, "w3_w0", 14), held([P, 512], U32, "w3_w1")]
         w3_s = [held([P, 512], U8, f"w3_s{g}") for g in range(2)]
 
         def prepare_w3(g):
-            signed = landed([P, 4, 512], BF16, f"w3_signed{g}", 1)
-            woven = keep.tile([P, 2048], BF16, name="w3_woven", align_bytes=64)
+            signed = landed([P, 4, 512], BF16, f"w3_signed{g}", 1 + 13 * g)
+            woven = landed([P, 2048], BF16, f"w3_woven{g}", 44)
             for j in range(4):
                 nc.scalar.activation(
                     out=signed[:, j, :].rearrange("p (u e m) -> p u m e", u=2, e=2),
@@ -180,11 +180,11 @@ def tile_list_block_face_features_kernel(
 
         h_w = held([P, S], U32, "h_w")
         h_s = held([P, S], U8, "h_s")
-        h_bf = []
+        h_bf = held([P, 4 * S], BF16, "h_bf")
 
-        def quantise_h(c):
-            cols = slice(128 * c, 128 * (c + 1))
-            nc.vector.quantize_mx(out=h_w[:, cols].bitcast(FP8X4), scales=h_s[:, cols], in_=h_bf[c][:])
+        def quantise_h(c0, c1):
+            cols = slice(128 * c0, 128 * c1)
+            nc.vector.quantize_mx(out=h_w[:, cols].bitcast(FP8X4), scales=h_s[:, cols], in_=h_bf[:, 512 * c0 : 512 * c1])
 
         for c in range(8):
             cols = slice(128 * c, 128 * (c + 1))
@@ -200,23 +200,24 @@ def tile_list_block_face_features_kernel(
                         start=(a == 0 and t == 0),
                         stop=(a == 1 and t == 3),
                     )
-            h_bf.append(ring.tile([P, 512], BF16, name="h_bf", align_bytes=64))
             in_half = slice(128 * (c % 4), 128 * (c % 4 + 1))
             nc.vector.tensor_tensor(
-                out=h_bf[c][:].rearrange("p (n i t) -> p n t i", i=2, t=4),
+                out=h_bf[:, 512 * c : 512 * (c + 1)].rearrange("p (n i t) -> p n t i", i=2, t=4),
                 in0=bank[:].rearrange("p t (n i) -> p n t i", i=2),
                 in1=abs_b[c // 4][:, :, in_half].rearrange("p t (n i) -> p n t i", i=2),
                 op=ALU.mult,
             )
-            if c > 0:
-                quantise_h(c - 1)
+            if c == 4:
+                quantise_h(0, 4)
+            if c == 6:
+                quantise_h(4, 6)
         quantise_w3(0, woven0)
-        quantise_h(7)
+        quantise_h(6, 8)
 
         g2 = {}
 
         def second_stage(g, t):
-            g2[g, t] = keep.tile([P, S], F32, name="g2", bufs=6)
+            g2[g, t] = keep.tile([P, S], F32, name="g2", bufs=8)
             for half in range(2):
                 cols = slice(512 * half, 512 * (half + 1))
                 bank = psum.tile([P, 512], F32, name="bank", bufs=8)
@@ -235,68 +236,67 @@ def tile_list_block_face_features_kernel(
 
         y_w = held([P, 2, M], U32, "y_w")
         y_s = held([P, 2, M], U8, "y_s")
-        pieces = [(0, 0, 512), (1, 0, 256), (1, 256, 512)]
+        pieces = [(0, 0, 512), (1, 0, 384), (1, 384, 512)]
+        last = len(pieces) - 1
         y = [held([P, 4, m1 - m0], F32, f"y{g}_{m0}") for g, m0, m1 in pieces]
-        larger = {}
+        y_bf = [held([P, 4 * (m1 - m0)], BF16, f"y_bf{g}_{m0}") for g, m0, m1 in pieces]
 
-        def pick_partner(k, t):
+        def pair_up(k):
             g, m0, m1 = pieces[k]
-            larger[k, t] = ring.tile([P, m1 - m0], F32, name="larger")
-            nc.vector.tensor_copy(out=larger[k, t][:], in_=g2[g, t][:].indirect(pos2_t[:, m0 // 16 : m1 // 16]))
-
-        def take_max(k, t):
-            g, m0, m1 = pieces[k]
-            nc.vector.tensor_tensor(out=larger[k, t][:], in0=larger[k, t][:], in1=base_t[g][:, t, m0:m1], op=ALU.max)
-
-        def finish(k, t):
-            g, m0, m1 = pieces[k]
-            nc.vector.tensor_tensor(
-                out=y[k][:, t, :], in0=g2[g, t][:].indirect(pos1_t[:, m0 // 16 : m1 // 16]), in1=larger[k, t][:], op=ALU.subtract
-            )
+            entries = slice(m0 // 16, m1 // 16)
             rows = out_0[512 * g : 512 * (g + 1), m0:m1].rearrange("(p t) m -> p t m", t=4)
-            nc.sync.dma_start(out=rows[:, t, :], in_=y[k][:, t, :])
-
-        y_bf = {}
+            for u in range(2):
+                partner = ring.tile([P, 2, m1 - m0], F32, name="partner")
+                larger = landed([P, 2, m1 - m0], F32, f"larger{k}_{u}", 48 - 4 * u)
+                for e in range(2):
+                    nc.vector.tensor_copy(out=partner[:, e, :], in_=g2[g, 2 * u + e][:].indirect(pos2_t[:, entries]))
+                nc.vector.tensor_tensor(
+                    out=larger[:], in0=partner[:], in1=base_t[g][:, 2 * u : 2 * u + 2, m0:m1], op=ALU.max
+                )
+                for e in range(2):
+                    t = 2 * u + e
+                    nc.vector.tensor_tensor(
+                        out=y[k][:, t, :],
+                        in0=g2[g, t][:].indirect(pos1_t[:, entries]),
+                        in1=larger[:, e, :],
+                        op=ALU.subtract,
+                    )
+                    if k < last:
+                        nc.sync.dma_start(out=rows[:, t, :], in_=y[k][:, t, :])
+                if k > 0 and u == 1:
+                    quantise_y(k - 1)
+            if k == last:
+                nc.sync.dma_start(out=rows, in_=y[k][:])
 
         def round_y(k):
-            g, m0, m1 = pieces[k]
-            y_bf[k] = held([P, 4 * (m1 - m0)], BF16, f"y_bf{k}")
             dst = y_bf[k][:].rearrange("p (c i t) -> p c t i", i=2, t=4)
             src = y[k][:].rearrange("p t (c i) -> p c t i", i=2)
-            if k == len(pieces) - 1:
+            if k == last:
                 nc.vector.tensor_copy(out=dst, in_=src)
             else:
                 nc.scalar.copy(out=dst, in_=src)
 
         def quantise_y(k):
             g, m0, m1 = pieces[k]
-            nc.vector.quantize_mx(out=y_w[:, g, m0:m1].bitcast(FP8X4), scales=y_s[:, g, m0:m1], in_=y_bf[k][:])
+            for c0 in range(m0, m1, 256):
+                c1 = min(c0 + 256, m1)
+                nc.vector.quantize_mx(
+                    out=y_w[:, g, c0:c1].bitcast(FP8X4),
+                    scales=y_s[:, g, c0:c1],
+                    in_=y_bf[k][:, 4 * (c0 - m0) : 4 * (c1 - m0)],
+                )
             words = out_1[g].rearrange("p m t -> p (m t)").bitcast(I32)
             nc.sync.dma_start(out=words[:, m0:m1], in_=y_w[:, g, m0:m1].bitcast(I32))
 
-        for t in range(2):
+        for t in range(4):
             second_stage(0, t)
         quantise_w3(1, prepare_w3(1))
-        for t in range(2, 4):
-            second_stage(0, t)
-        for t in range(2):
+        for t in range(4):
             second_stage(1, t)
-
-        steps = [(k, t) for k in range(len(pieces)) for t in range(4)]
-        for i, (k, t) in enumerate(steps):
-            pick_partner(k, t)
-            if i > 0:
-                finish(*steps[i - 1])
-            take_max(k, t)
-            if i in (1, 2):
-                second_stage(1, i + 1)
-            if k > 0 and t == 0:
-                round_y(k - 1)
-            if k > 0 and t == 3:
-                quantise_y(k - 1)
-        finish(*steps[-1])
-        round_y(len(pieces) - 1)
-        quantise_y(len(pieces) - 1)
+        for k in range(len(pieces)):
+            pair_up(k)
+            round_y(k)
+        quantise_y(last)
         for q in range(4):
             queue = nc.scalar if q % 2 else nc.sync
             queue.dma_start(

from contextlib import ExitStack

import concourse.mybir as mybir

K, H, N, T, S, M = 1024, 512, 1024, 4096, 1024, 512
FLOPS = 2 * (2 * K * H * S + H * N * S)

F32 = mybir.dt.float32
BF16 = mybir.dt.bfloat16
I32 = mybir.dt.int32
U32 = mybir.dt.uint32
U16 = mybir.dt.uint16
U8 = mybir.dt.uint8
FP8X4 = mybir.dt.float8_e4m3fn_x4
FP4X4 = mybir.dt.float4_e2m1fn_x4
ALU = mybir.AluOpType
ACT = mybir.ActivationFunctionType
P = 128


def tile_list_block_face_features_kernel(
    tc, tab_words, tab_scales, offs, wa, wb_words, wb_scales, gain, w3, thr, pos1, pos2, base, out_0, out_1, out_2
):
    nc = tc.nc
    with ExitStack() as ctx:
        keep = ctx.enter_context(tc.tile_pool(name="keep", bufs=1))
        ring = ctx.enter_context(tc.tile_pool(name="ring", bufs=3))
        loads = ctx.enter_context(tc.tile_pool(name="loads", bufs=1))
        psum = ctx.enter_context(tc.psum_pool(name="psum", bufs=1))

        def held(shape, dtype, name):
            return keep.tile(shape, dtype, name=name, align_bytes=64)

        def landed(shape, dtype, name, kib):
            return loads.tile(shape, dtype, name=name, offset=1024 * kib, align_bytes=64)

        offs_t = held([P, S // 16], U16, "offs_t")
        pos1_t = held([P, M // 16], U16, "pos1_t")
        pos2_t = held([P, M // 16], U16, "pos2_t")
        wb_w_raw = landed([P, 2, 2 * H], U8, "wb_w_raw", 31)
        tab_w = [landed([P, T], I32, f"tab_w{a}", 16 * a) for a in range(2)]
        tab_s = landed([P, T], U8, "tab_s", 40)
        v_w = [held([P, S], U32, f"v_w{a}") for a in range(2)]
        v_s = [landed([P, S], U8, "v_s0", 0), held([P, S], U8, "v_s1")]
        wb_s_raw = held([P, 2, H], U8, "wb_s_raw")
        wb_w = held([P, 2, 2 * H], U8, "wb_w")
        wb_s = landed([P, 2, H], U8, "wb_s", 1)
        gain_t = held([P, 4], F32, "gain_t")
        thr_t = held([P, 2, 4], F32, "thr_t")

        nc.vector.memset(tab_s[:].bitcast(I32), 0)
        nc.gpsimd.memset(wb_s_raw[:].rearrange("p a c -> p (a c)").bitcast(I32), 0)
        nc.gpsimd.memset(v_s[1][:].bitcast(I32), 0)

        tab_rows = [tab_words[a].rearrange("p t i -> p (t i)").bitcast(I32) for a in range(2)]
        nc.sync.dma_start(offs_t[:], offs)
        nc.scalar.dma_start(out=wb_w_raw[:].bitcast(I32), in_=wb_words.rearrange("a p c -> p a c").bitcast(I32))
        nc.gpsimd.dma_start(out=gain_t[:], in_=gain.rearrange("(p t) -> p t", t=4))
        nc.gpsimd.dma_start(out=thr_t[:], in_=thr.rearrange("(g p t) -> p g t", g=2, t=4))
        nc.sync.dma_start(pos2_t[:], pos2)
        nc.sync.dma_start(pos1_t[:], pos1)
        wa_parts = [(0, 0, H, 32), (1, 0, H // 2, 2), (1, H // 2, H, 6)]
        wa_raw = [landed([P, 4, c1 - c0], F32, f"wa_raw{a}_{c0}", kib) for a, c0, c1, kib in wa_parts]
        wa_bf = [landed([P, 4 * H], BF16, f"wa_bf{a}", 16) for a in range(2)]
        wa_w = [held([P, H], U32, f"wa_w{a}") for a in range(2)]
        wa_s = [held([P, H], U8, f"wa_s{a}") for a in range(2)]

        def load_wa(i):
            a, c0, c1, kib = wa_parts[i]
            rows = wa[512 * a : 512 * (a + 1), c0:c1].rearrange("(p j) c -> p j c", j=4)
            nc.sync.dma_start(out=wa_raw[i][:], in_=rows)

        def prepare_wa(i):
            a, c0, c1, kib = wa_parts[i]
            nc.vector.tensor_copy(
                out=wa_bf[a][:].rearrange("p (u e m j) -> p u m j e", u=2, e=2, j=4)[:, :, c0 // 4 : c1 // 4, :, :],
                in_=wa_raw[i][:].rearrange("p j (m u e) -> p u m j e", u=2, e=2),
            )
            if c1 == H:
                for t in range(4):
                    nc.vector.quantize_mx(
                        out=wa_w[a][:, 128 * t : 128 * (t + 1)].bitcast(FP8X4),
                        scales=wa_s[a][:, 128 * t : 128 * (t + 1)],
                        in_=wa_bf[a][:, 512 * t : 512 * (t + 1)],
                    )

        for q in range(4):
            if q == 2:
                nc.sync.dma_start(out=tab_w[0][:], in_=tab_rows[0])
            nc.sync.dma_start(
                out=wb_s_raw[32 * q : 32 * q + 4, :, :].bitcast(I32),
                in_=wb_scales[:, 4 * q : 4 * q + 4, :].rearrange("a r c -> r a c").bitcast(I32),
            )
        for q in range(4):
            nc.sync.dma_start(
                out=tab_s[32 * q : 32 * q + 8, :].bitcast(I32), in_=tab_scales[:, 4 * q : 4 * q + 4, :].bitcast(I32)
            )
        for a in range(2):
            nc.vector.tensor_copy(
                out=wb_w[:, a, :].rearrange("p (t m b) -> p t m b", t=4, b=2),
                in_=wb_w_raw[:, a, :].rearrange("p (m t b) -> p t m b", t=4, b=2),
            )
        nc.sync.dma_start(out=tab_w[1][:], in_=tab_rows[1])
        load_wa(0)
        nc.vector.tensor_copy(out=v_w[0][:], in_=tab_w[0][:].bitcast(U32).indirect(offs_t[:]))
        load_wa(1)
        load_wa(2)
        nc.vector.tensor_copy(
            out=wb_s[:].rearrange("p a (t m) -> p a t m", t=4), in_=wb_s_raw[:].rearrange("p a (m t) -> p a t m", t=4)
        )
        nc.vector.tensor_copy(out=v_s[0][:], in_=tab_s[:].indirect(offs_t[:]))
        for q in range(4):
            nc.scalar.dma_start(
                out=v_s[1][32 * q : 32 * q + 4, :].bitcast(I32), in_=v_s[0][32 * q + 4 : 32 * q + 8, :].bitcast(I32)
            )
        for half in range(2):
            nc.vector.tensor_copy(
                out=v_w[1][:, 512 * half : 512 * (half + 1)],
                in_=tab_w[1][:].bitcast(U32).indirect(offs_t[:, 32 * half : 32 * (half + 1)]),
            )

        w3_raw = [[landed([P, 2, 512], F32, f"w3_raw{g}_{u}", [[40, 28], [20, 24]][g][u]) for u in range(2)] for g in range(2)]
        base_t = [landed([P, 4, M], F32, f"base{g}", 32 - 26 * g) for g in range(2)]
        w3_rows = w3.rearrange("(p j) n -> p j n", j=4)
        for g in range(2):
            for u in range(2):
                nc.sync.dma_start(out=w3_raw[g][u][:], in_=w3_rows[:, 2 * u : 2 * u + 2, 512 * g : 512 * (g + 1)])
            nc.sync.dma_start(out=base_t[g][:], in_=base[512 * g : 512 * (g + 1), :].rearrange("(p t) m -> p t m", t=4))

        sign_01 = held([P, 4], F32, "sign_01")
        sign_t = held([P, 4], F32, "sign_t")
        neg_thr = held([P, 2, 4], F32, "neg_thr")
        nc.gpsimd.tensor_scalar(out=sign_01[:], in0=gain_t[:], scalar1=0.0, scalar2=2.0, op0=ALU.is_ge, op1=ALU.mult)
        nc.gpsimd.tensor_scalar(out=sign_t[:], in0=sign_01[:], scalar1=1.0, scalar2=-1.0, op0=ALU.mult, op1=ALU.add)
        nc.gpsimd.tensor_scalar(out=neg_thr[:], in0=thr_t[:], scalar1=-1.0, scalar2=0.0, op0=ALU.mult, op1=ALU.add)

        abs_b = [held([P, 4, 512], F32, f"abs_b{half}") for half in range(2)]
        for half in range(2):
            cols = slice(512 * half, 512 * (half + 1))
            for t in range(4):
                bank = psum.tile([P, 512], F32, name="bank", bufs=8)
                for a in range(2):
                    nc.tensor.matmul_mx(
                        out=bank[:],
                        lhsT=wb_w[:, a, 256 * t : 256 * (t + 1)].bitcast(FP4X4),
                        lhsT_scale=wb_s[:, a, 128 * t : 128 * (t + 1)],
                        rhs=v_w[a][:, cols].bitcast(FP8X4),
                        rhs_scale=v_s[a][:, cols],
                        start=(a == 0),
                        stop=(a == 1),
                    )
                nc.scalar.activation(out=abs_b[half][:, t, :], in_=bank[:], func=ACT.Abs, scale=gain_t[:, t : t + 1])

        for i in range(3):
            prepare_wa(i)

        w3_w = [landed([P, 512], U32, "w3_w0", 14), held([P, 512], U32, "w3_w1")]
        w3_s = [held([P, 512], U8, f"w3_s{g}") for g in range(2)]

        def prepare_w3(g):
            signed = landed([P, 4, 512], BF16, f"w3_signed{g}", 1 + 13 * g)
            woven = landed([P, 2048], BF16, f"w3_woven{g}", 44)
            for j in range(4):
                nc.scalar.activation(
                    out=signed[:, j, :].rearrange("p (u e m) -> p u m e", u=2, e=2),
                    in_=w3_raw[g][j // 2][:, j % 2, :].rearrange("p (m u e) -> p u m e", u=2, e=2),
                    func=ACT.Copy,
                    scale=sign_t[:, j : j + 1],
                )
            nc.scalar.copy(
                out=woven[:].rearrange("p (c i j) -> p c j i", i=4, j=4),
                in_=signed[:].rearrange("p j (c i) -> p c j i", i=4),
            )
            return woven

        def quantise_w3(g, woven):
            nc.vector.quantize_mx(out=w3_w[g][:].bitcast(FP8X4), scales=w3_s[g][:], in_=woven[:])

        woven0 = prepare_w3(0)

        h_w = held([P, S], U32, "h_w")
        h_s = held([P, S], U8, "h_s")
        h_bf = held([P, 4 * S], BF16, "h_bf")

        def quantise_h(c0, c1):
            cols = slice(128 * c0, 128 * c1)
            nc.vector.quantize_mx(out=h_w[:, cols].bitcast(FP8X4), scales=h_s[:, cols], in_=h_bf[:, 512 * c0 : 512 * c1])

        for c in range(8):
            cols = slice(128 * c, 128 * (c + 1))
            bank = psum.tile([P, 4, 128], F32, name="bank", bufs=8)
            for a in range(2):
                for t in range(4):
                    nc.tensor.matmul_mx(
                        out=bank[:, t, :],
                        lhsT=wa_w[a][:, 128 * t : 128 * (t + 1)].bitcast(FP8X4),
                        lhsT_scale=wa_s[a][:, 128 * t : 128 * (t + 1)],
                        rhs=v_w[a][:, cols].bitcast(FP8X4),
                        rhs_scale=v_s[a][:, cols],
                        start=(a == 0 and t == 0),
                        stop=(a == 1 and t == 3),
                    )
            in_half = slice(128 * (c % 4), 128 * (c % 4 + 1))
            nc.vector.tensor_tensor(
                out=h_bf[:, 512 * c : 512 * (c + 1)].rearrange("p (n i t) -> p n t i", i=2, t=4),
                in0=bank[:].rearrange("p t (n i) -> p n t i", i=2),
                in1=abs_b[c // 4][:, :, in_half].rearrange("p t (n i) -> p n t i", i=2),
                op=ALU.mult,
            )
            if c == 4:
                quantise_h(0, 4)
            if c == 6:
                quantise_h(4, 6)
        quantise_w3(0, woven0)
        quantise_h(6, 8)

        g2 = {}

        def second_stage(g, t):
            g2[g, t] = keep.tile([P, S], F32, name="g2", bufs=8)
            for half in range(2):
                cols = slice(512 * half, 512 * (half + 1))
                bank = psum.tile([P, 512], F32, name="bank", bufs=8)
                nc.tensor.matmul_mx(
                    out=bank[:],
                    lhsT=w3_w[g][:, 128 * t : 128 * (t + 1)].bitcast(FP8X4),
                    lhsT_scale=w3_s[g][:, 128 * t : 128 * (t + 1)],
                    rhs=h_w[:, cols].bitcast(FP8X4),
                    rhs_scale=h_s[:, cols],
                    start=True,
                    stop=True,
                )
                nc.scalar.activation(
                    out=g2[g, t][:, cols], in_=bank[:], func=ACT.Gelu_apprx_tanh, bias=neg_thr[:, g, t : t + 1]
                )

        y_w = held([P, 2, M], U32, "y_w")
        y_s = held([P, 2, M], U8, "y_s")
        pieces = [(0, 0, 512), (1, 0, 384), (1, 384, 512)]
        last = len(pieces) - 1
        y = [held([P, 4, m1 - m0], F32, f"y{g}_{m0}") for g, m0, m1 in pieces]
        y_bf = [held([P, 4 * (m1 - m0)], BF16, f"y_bf{g}_{m0}") for g, m0, m1 in pieces]

        def pair_up(k):
            g, m0, m1 = pieces[k]
            entries = slice(m0 // 16, m1 // 16)
            rows = out_0[512 * g : 512 * (g + 1), m0:m1].rearrange("(p t) m -> p t m", t=4)
            for u in range(2):
                partner = ring.tile([P, 2, m1 - m0], F32, name="partner")
                larger = landed([P, 2, m1 - m0], F32, f"larger{k}_{u}", 48 - 4 * u)
                for e in range(2):
                    nc.vector.tensor_copy(out=partner[:, e, :], in_=g2[g, 2 * u + e][:].indirect(pos2_t[:, entries]))
                nc.vector.tensor_tensor(
                    out=larger[:], in0=partner[:], in1=base_t[g][:, 2 * u : 2 * u + 2, m0:m1], op=ALU.max
                )
                for e in range(2):
                    t = 2 * u + e
                    nc.vector.tensor_tensor(
                        out=y[k][:, t, :],
                        in0=g2[g, t][:].indirect(pos1_t[:, entries]),
                        in1=larger[:, e, :],
                        op=ALU.subtract,
                    )
                    if k < last:
                        nc.sync.dma_start(out=rows[:, t, :], in_=y[k][:, t, :])
                if k > 0 and u == 1:
                    quantise_y(k - 1)
            if k == last:
                nc.sync.dma_start(out=rows, in_=y[k][:])

        def round_y(k):
            dst = y_bf[k][:].rearrange("p (c i t) -> p c t i", i=2, t=4)
            src = y[k][:].rearrange("p t (c i) -> p c t i", i=2)
            if k == last:
                nc.vector.tensor_copy(out=dst, in_=src)
            else:
                nc.scalar.copy(out=dst, in_=src)

        def quantise_y(k):
            g, m0, m1 = pieces[k]
            for c0 in range(m0, m1, 256):
                c1 = min(c0 + 256, m1)
                nc.vector.quantize_mx(
                    out=y_w[:, g, c0:c1].bitcast(FP8X4),
                    scales=y_s[:, g, c0:c1],
                    in_=y_bf[k][:, 4 * (c0 - m0) : 4 * (c1 - m0)],
                )
            words = out_1[g].rearrange("p m t -> p (m t)").bitcast(I32)
            nc.sync.dma_start(out=words[:, m0:m1], in_=y_w[:, g, m0:m1].bitcast(I32))

        for t in range(4):
            second_stage(0, t)
        quantise_w3(1, prepare_w3(1))
        for t in range(4):
            second_stage(1, t)
        for k in range(len(pieces)):
            pair_up(k)
            round_y(k)
        quantise_y(last)
        for q in range(4):
            queue = nc.scalar if q % 2 else nc.sync
            queue.dma_start(
                out=out_2[:, 4 * q : 4 * q + 4, :].rearrange("g r m -> r g m").bitcast(I32),
                in_=y_s[32 * q : 32 * q + 4, :, :].bitcast(I32),
            )
